import numpy as np, ml_dtypes
CORES = [16,17,18,19,150,151]
N = 6
import mx_ref
NC, G = 128, 2
C = np.float32(0.031)
BF = ml_dtypes.bfloat16
def cut(t, i, w=512):
    return t[:, w * i:w * i + w]
def tile(rs):
    return np.stack(rs, axis=2).reshape(128, -1).astype(BF)
def layer(w, X):
    out = []
    for i in range(G):
        for t in range(len(X)):
            p = mx_ref.matmul(mx_ref.quantize(cut(w, len(X) * i + t)), X[t])
            z = p if t == 0 else z + p
        out.append(z)
    return out
def act(Z):
    return [np.maximum(s * z, 0) * C for z in Z for s in (1, -1)]
def pick(b):
    s = np.zeros((128, 128, 4), np.float32)
    s[np.arange(128), np.arange(128), b] = 1.0
    return mx_ref.quantize(s.reshape(128, 512).astype(BF))
def setup_inputs(rng):
    def f(*shape):
        return mx_ref.flush((rng.standard_normal(shape, dtype=np.float32) * np.exp2(rng.integers(-2, 3, shape[:-1] + (1,)))).astype(BF))
    return {"a": f(N, 128, G * 512), "b": f(N, 128, N * 4 * NC)}
def setup_inputs_blocks(rng):
    d = setup_inputs(rng)
    for k in ("a", "b"): d[k] = mx_ref.spread(d[k], rng, 4)
    return d
def setup_inputs_wide(rng):
    d = setup_inputs(rng)
    for k in ("a", "b"): d[k] = mx_ref.flush((d[k].astype(np.float32) * np.exp2(rng.integers(-8, 9, (N, 1, 1))).astype(np.float32)).astype(BF))
    return d
def reference(a, b):
    S = [pick(t) for t in range(4)]
    y = np.zeros((N, 128, NC, 4), np.float32)
    for c in range(N):
        for k in range(1, N + 1):
            r = (c + k) % N
            R = act(layer(a[r], [mx_ref.quantize(cut(b[r], c, 4 * NC))]))
            if k > 1: R = [R[t] + mx_ref.matmul(S[t], q) for t in range(4)]
            if k < N: q = mx_ref.quantize(tile(R))
        y[c] = np.stack(R, axis=2)
    return {"y": y.reshape(N, 128, 4 * NC)}

@@ -1,0 +1,177 @@
+from concourse.mybir import dt, AluOpType, ActivationFunctionType
+
+N = 6
+W = 512
+NC = 128
+C = 0.031
+NS = N - 1
+
+SCRATCH = {
+    "abf": ("sbuf", [128, 2 * W], "bfloat16"),
+    "bbf": ("sbuf", [128, N * W], "bfloat16"),
+    "aq": ("sbuf", [128, 2 * NC], "float8_e4m3fn_x4"),
+    "asc": ("sbuf", [128, 2 * NC], "uint8"),
+    "bq": ("sbuf", [128, N * NC], "float8_e4m3fn_x4"),
+    "bsc": ("sbuf", [128, N * NC], "uint8"),
+    "wbf": ("sbuf", [128, W + 4], "bfloat16"),
+    "sq": ("sbuf", [128, 4 * NC], "float8_e4m3fn_x4"),
+    "ssc": ("sbuf", [128, 4 * NC], "uint8"),
+    "rf": ("sbuf", [128, 4 * NS * NC], "float32"),
+    "tbf": ("sbuf", [128, NS * W], "bfloat16"),
+    "tq": ("sbuf", [128, NS * NC], "float8_e4m3fn_x4"),
+    "tsc": ("sbuf", [128, NS * NC], "uint8"),
+    "lq": ("sbuf", [128, NS * NC], "float8_e4m3fn_x4"),
+    "lsc": ("sbuf", [128, NS * NC], "uint8"),
+    "yf": ("sbuf", [128, W], "float32"),
+    "pz": ("psum", [128, 4 * 512], "float32"),
+    "pd": ("psum", [128, 4 * 512], "float32"),
+}
+
+SEMAPHORES = (
+    ["la", "ones", "wsel", "qa0", "qa1", "act1", "qs", "add", "qt", "sent", "ydone"]
+    + ["lb%d" % i for i in (1, 2, 3, 4)]
+    + ["qb%d" % i for i in (1, 2, 3, 4)]
+    + ["z%d%d" % (i, j) for i in (1, 2, 3, 4) for j in (0, 1)]
+    + ["r%d" % i for i in (2, 3, 4)]
+    + ["d%d" % b for b in range(4)]
+    + ["arr%d" % k for k in range(1, N)]
+)
+
+GROUP = {1: (5, 6), 2: (4, 5), 3: (2, 4), 4: (0, 2)}
+BANK = {1: 0, 2: 2, 3: 0, 4: 2}
+GROUP_OF_STEP = {1: 1, 2: 2, 3: 3, 4: 3, 5: 4, 6: 4}
+
+
+def _count(mask):
+    return sum((mask >> e) & 1 for e in range(16))
+
+
+def rank_program(g, core, T, topo):
+    r = T.rank_of(core)
+    if r is None:
+        return
+    sem = T.sem
+    v, pe, sc, sy = g.vector, g.tensor, g.scalar, g.sync
+    nxt, prv = T.cores[(r + 1) % N], T.cores[(r - 1) % N]
+    out_mask = topo.mask(core, nxt)
+    n_out, n_in = _count(out_mask), _count(topo.mask(prv, core))
+    rid, pid = topo.addr(nxt, core)
+    relu = ActivationFunctionType.Relu
+
+    def load(queue, gi):
+        s0, s1 = GROUP[gi]
+        n, s = 0, s0
+        while s < s1:
+            c, e = (r + s) % N, s + 1
+            while e < s1 and (r + e) % N == c + (e - s):
+                e += 1
+            queue.dma_start(T.bbf[:, W * s:W * e], T.b[:, W * c:W * (c + e - s)]).then_inc(sem["lb%d" % gi], 16)
+            n, s = n + 16, e
+        return n
+
+    def quant_b(gi):
+        s0, s1 = GROUP[gi]
+        v.wait_ge(sem["lb%d" % gi], loaded[gi])
+        v.quantize_mx(T.bq[:, NC * s0:NC * s1], T.bsc[:, NC * s0:NC * s1],
+                      T.bbf[:, W * s0:W * s1]).then_inc(sem["qb%d" % gi], 1)
+
+    def zview(gi, i):
+        s0, s1 = GROUP[gi]
+        col = 512 * (BANK[gi] + i)
+        return T.pz[:, col:col + NC * (s1 - s0)]
+
+    def products(gi):
+        s0, s1 = GROUP[gi]
+        pe.wait_ge(sem["qb%d" % gi], 1)
+        for i in (0, 1):
+            if gi == 1:
+                pe.wait_ge(sem["qa%d" % i], 1)
+            pe.matmul_mx(zview(gi, i), T.aq[:, NC * i:NC * (i + 1)], T.asc[:, NC * i:NC * (i + 1)],
+                         T.bq[:, NC * s0:NC * s1], T.bsc[:, NC * s0:NC * s1], True, True).then_inc(sem["z%d%d" % (gi, i)], 1)
+
+    def rview(b, s0, s1):
+        return T.rf[:, NS * NC * b + NC * s0:NS * NC * b + NC * s1]
+
+    def parts(gi):
+        s0, s1 = GROUP[gi]
+        for i in (0, 1):
+            sc.wait_ge(sem["z%d%d" % (gi, i)], 1)
+            for j, f in ((0, C), (1, -C)):
+                sc.activation(rview(2 * i + j, s0, s1), zview(gi, i), relu, scale=f).then_inc(sem["r%d" % gi], 1)
+
+    loaded = {}
+    sy.dma_start(T.abf[:], T.a[:]).then_inc(sem.la, 16)
+    loaded[1] = load(sc, 1)
+    loaded[2] = load(sy, 2)
+    loaded[3] = load(sc, 3)
+    loaded[4] = load(sy, 4)
+
+    v.memset(T.wbf[:], 1.0).then_inc(sem.ones, 1)
+    g.wait_ge(sem.ones, 1)
+    g.affine_select(T.wbf[:], T.wbf[:], [[-1, W + 4]], AluOpType.is_equal, 0.0, 3, 4).then_inc(sem.wsel, 1)
+
+    quant_b(1)
+    v.wait_ge(sem.la, 16)
+    for i in (0, 1):
+        v.quantize_mx(T.aq[:, NC * i:NC * (i + 1)], T.asc[:, NC * i:NC * (i + 1)],
+                      T.abf[:, W * i:W * (i + 1)]).then_inc(sem["qa%d" % i], 1)
+    products(1)
+    v.wait_ge(sem.z10, 1)
+    v.tensor_scalar(T.tbf[:, 0:W:4], zview(1, 0), 0.0, C, AluOpType.max, AluOpType.mult).then_inc(sem.act1, 1)
+    v.tensor_scalar(T.tbf[:, 1:W:4], zview(1, 0), -C, 0.0, AluOpType.mult, AluOpType.max).then_inc(sem.act1, 1)
+    sc.wait_ge(sem.z11, 1)
+    sc.activation(T.tbf[:, 2:W:4], zview(1, 1), relu, scale=C).then_inc(sem.act1, 1)
+    sc.activation(T.tbf[:, 3:W:4], zview(1, 1), relu, scale=-C).then_inc(sem.act1, 1)
+    v.wait_ge(sem.act1, 4)
+    v.quantize_mx(T.tq[:, 0:NC], T.tsc[:, 0:NC], T.tbf[:, 0:W]).then_inc(sem.qt, 1)
+
+    quant_b(2)
+    products(2)
+    parts(2)
+    v.wait_ge(sem.wsel, 1)
+    for b in range(4):
+        v.quantize_mx(T.sq[:, NC * b:NC * (b + 1)], T.ssc[:, NC * b:NC * (b + 1)],
+                      T.wbf[:, 3 - b:3 - b + W]).then_inc(sem.qs, 1)
+    quant_b(3)
+    pe.wait_ge(sem.act1, 4)
+    products(3)
+    parts(3)
+
+    for k in range(2, N + 1):
+        s = N - k
+        lo, hi = NC * (k - 2), NC * (k - 1)
+        pe.wait_ge(sem["arr%d" % (k - 1)], 2 * n_in)
+        if k == 2:
+            pe.wait_ge(sem.qs, 4)
+        else:
+            pe.wait_ge(sem.add, 4 * (k - 2))
+        for b in range(4):
+            pe.matmul_mx(T.pd[:, 512 * b:512 * b + NC], T.sq[:, NC * b:NC * (b + 1)], T.ssc[:, NC * b:NC * (b + 1)],
+                         T.lq[:, lo:hi], T.lsc[:, lo:hi], True, True).then_inc(sem["d%d" % b], 1)
+        v.wait_ge(sem["r%d" % GROUP_OF_STEP[k]], 4)
+        for b in range(4):
+            out = T.tbf[:, W * (k - 1) + b:W * k:4] if k < N else T.yf[:, b:W:4]
+            v.wait_ge(sem["d%d" % b], k - 1)
+            v.tensor_tensor(out, T.pd[:, 512 * b:512 * b + NC], rview(b, s, s + 1), AluOpType.add).then_inc(sem.add, 1)
+        if k < N:
+            v.wait_ge(sem.add, 4 * (k - 1))
+            v.quantize_mx(T.tq[:, NC * (k - 1):NC * k], T.tsc[:, NC * (k - 1):NC * k],
+                          T.tbf[:, W * (k - 1):W * k]).then_inc(sem.qt, 1)
+        if k == 2:
+            quant_b(4)
+            pe.wait_ge(sem.r2, 4)
+            products(4)
+            parts(4)
+
+    for k in range(1, N):
+        lo, hi = NC * (k - 1), NC * k
+        g.wait_ge(sem.qt, k)
+        g.remote_dma(out_ap=T.lq[:, lo:hi].bitcast(dt.uint8), in_ap=T.tq[:, lo:hi].bitcast(dt.uint8),
+                     remote_sem=sem["arr%d" % k], local_sem=sem.sent, pid=pid, routing_id=rid, dma_engine_mask=out_mask)
+        g.remote_dma(out_ap=T.lsc[:, lo:hi], in_ap=T.tsc[:, lo:hi],
+                     remote_sem=sem["arr%d" % k], local_sem=sem.sent, pid=pid, routing_id=rid, dma_engine_mask=out_mask)
+
+    sy.wait_ge(sem.add, 4 * (N - 1))
+    sy.dma_start(T.y[:], T.yf[:]).then_inc(sem.ydone, 16)
+    sy.wait_ge(sem.ydone, 16)
+    g.wait_ge(sem.sent, 2 * n_out * (N - 1))

@@ -13,9 +13,14 @@ SCRATCH = {
     "asc": ("sbuf", [128, 2 * NC], "uint8"),
     "bq": ("sbuf", [128, N * NC], "float8_e4m3fn_x4"),
     "bsc": ("sbuf", [128, N * NC], "uint8"),
+    "pmj": ("sbuf", [128, NC], "float32"),
     "wbf": ("sbuf", [128, W + 4], "bfloat16"),
-    "sq": ("sbuf", [128, 4 * NC], "float8_e4m3fn_x4"),
-    "ssc": ("sbuf", [128, 4 * NC], "uint8"),
+    "sq": ("sbuf", [128, 3 * NC], "float8_e4m3fn_x4"),
+    "ssc": ("sbuf", [128, 3 * NC], "uint8"),
+    "xq": ("sbuf", [128, NC], "float8_e4m3fn_x4"),
+    "xsc": ("sbuf", [128, NC], "uint8"),
+    "pq": ("sbuf", [128, NC], "float8_e4m3fn_x4"),
+    "psc": ("sbuf", [128, NC], "uint8"),
     "rf": ("sbuf", [128, 4 * NS * NC], "float32"),
     "tbf": ("sbuf", [128, NS * W], "bfloat16"),
     "tq": ("sbuf", [128, NS * NC], "float8_e4m3fn_x4"),
@@ -28,7 +33,7 @@ SCRATCH = {
 }
 
 SEMAPHORES = (
-    ["la", "ones", "wsel", "qa0", "qa1", "act1", "qs", "add", "qt", "sent", "ydone"]
+    ["la0", "la1", "iot", "zero", "wsel", "qx", "arrs", "qa0", "qa1", "act1", "qs", "add", "qt", "sent", "ydone"]
     + ["lb%d" % i for i in (1, 2, 3, 4)]
     + ["qb%d" % i for i in (1, 2, 3, 4)]
     + ["z%d%d" % (i, j) for i in (1, 2, 3, 4) for j in (0, 1)]
@@ -99,20 +104,38 @@ def rank_program(g, core, T, topo):
             for j, f in ((0, C), (1, -C)):
                 sc.activation(rview(2 * i + j, s0, s1), zview(gi, i), relu, scale=f).then_inc(sem["r%d" % gi], 1)
 
-    loaded = {}
-    sy.dma_start(T.abf[:], T.a[:]).then_inc(sem.la, 16)
-    loaded[1] = load(sc, 1)
-    loaded[2] = load(sy, 2)
-    loaded[3] = load(sc, 3)
-    loaded[4] = load(sy, 4)
+    def send(dq, dsc, q, s_, arrival):
+        g.remote_dma(out_ap=dq.bitcast(dt.uint8), in_ap=q.bitcast(dt.uint8),
+                     remote_sem=arrival, local_sem=sem.sent, pid=pid, routing_id=rid, dma_engine_mask=out_mask)
+        g.remote_dma(out_ap=dsc, in_ap=s_,
+                     remote_sem=arrival, local_sem=sem.sent, pid=pid, routing_id=rid, dma_engine_mask=out_mask)
 
-    v.memset(T.wbf[:], 1.0).then_inc(sem.ones, 1)
-    g.wait_ge(sem.ones, 1)
-    g.affine_select(T.wbf[:], T.wbf[:], [[-1, W + 4]], AluOpType.is_equal, 0.0, 3, 4).then_inc(sem.wsel, 1)
+    def pick(b):
+        if b < 3:
+            return T.sq[:, NC * b:NC * (b + 1)], T.ssc[:, NC * b:NC * (b + 1)]
+        return T.pq[:], T.psc[:]
+
+    loaded = {}
+    sy.dma_start(T.abf[:, 0:W], T.a[:, 0:W]).then_inc(sem.la0, 16)
+    loaded[1] = load(sc, 1)
+    sy.dma_start(T.abf[:, W:2 * W], T.a[:, W:2 * W]).then_inc(sem.la1, 16)
+    loaded[2] = load(sc, 2)
+    loaded[3] = load(sy, 3)
+    loaded[4] = load(sc, 4)
+
+    g.iota(T.pmj[:], [[-1, NC]], 0, 1, allow_small_or_imprecise_dtypes=True).then_inc(sem.iot, 1)
+    v.memset(T.wbf[:], 0.0).then_inc(sem.zero, 1)
+    v.wait_ge(sem.zero, 1)
+    v.wait_ge(sem.iot, 1)
+    v.tensor_scalar(T.wbf[:, 3:W + 3:4], T.pmj[:], 0.0, None, AluOpType.is_equal).then_inc(sem.wsel, 1)
+    v.wait_ge(sem.wsel, 1)
+    v.quantize_mx(T.xq[:], T.xsc[:], T.wbf[:, 0:W]).then_inc(sem.qx, 1)
+    g.wait_ge(sem.qx, 1)
+    send(T.pq[:], T.psc[:], T.xq[:], T.xsc[:], sem.arrs)
 
     quant_b(1)
-    v.wait_ge(sem.la, 16)
     for i in (0, 1):
+        v.wait_ge(sem["la%d" % i], 16)
         v.quantize_mx(T.aq[:, NC * i:NC * (i + 1)], T.asc[:, NC * i:NC * (i + 1)],
                       T.abf[:, W * i:W * (i + 1)]).then_inc(sem["qa%d" % i], 1)
     products(1)
@@ -128,10 +151,9 @@ def rank_program(g, core, T, topo):
     quant_b(2)
     products(2)
     parts(2)
-    v.wait_ge(sem.wsel, 1)
-    for b in range(4):
-        v.quantize_mx(T.sq[:, NC * b:NC * (b + 1)], T.ssc[:, NC * b:NC * (b + 1)],
-                      T.wbf[:, 3 - b:3 - b + W]).then_inc(sem.qs, 1)
+    for b in range(3):
+        q, s_ = pick(b)
+        v.quantize_mx(q, s_, T.wbf[:, 3 - b:3 - b + W]).then_inc(sem.qs, 1)
     quant_b(3)
     pe.wait_ge(sem.act1, 4)
     products(3)
@@ -142,11 +164,13 @@ def rank_program(g, core, T, topo):
         lo, hi = NC * (k - 2), NC * (k - 1)
         pe.wait_ge(sem["arr%d" % (k - 1)], 2 * n_in)
         if k == 2:
-            pe.wait_ge(sem.qs, 4)
+            pe.wait_ge(sem.qs, 3)
+            pe.wait_ge(sem.arrs, 2 * n_in)
         else:
             pe.wait_ge(sem.add, 4 * (k - 2))
         for b in range(4):
-            pe.matmul_mx(T.pd[:, 512 * b:512 * b + NC], T.sq[:, NC * b:NC * (b + 1)], T.ssc[:, NC * b:NC * (b + 1)],
+            q, s_ = pick(b)
+            pe.matmul_mx(T.pd[:, 512 * b:512 * b + NC], q, s_,
                          T.lq[:, lo:hi], T.lsc[:, lo:hi], True, True).then_inc(sem["d%d" % b], 1)
         v.wait_ge(sem["r%d" % GROUP_OF_STEP[k]], 4)
         for b in range(4):
@@ -166,12 +190,9 @@ def rank_program(g, core, T, topo):
     for k in range(1, N):
         lo, hi = NC * (k - 1), NC * k
         g.wait_ge(sem.qt, k)
-        g.remote_dma(out_ap=T.lq[:, lo:hi].bitcast(dt.uint8), in_ap=T.tq[:, lo:hi].bitcast(dt.uint8),
-                     remote_sem=sem["arr%d" % k], local_sem=sem.sent, pid=pid, routing_id=rid, dma_engine_mask=out_mask)
-        g.remote_dma(out_ap=T.lsc[:, lo:hi], in_ap=T.tsc[:, lo:hi],
-                     remote_sem=sem["arr%d" % k], local_sem=sem.sent, pid=pid, routing_id=rid, dma_engine_mask=out_mask)
+        send(T.lq[:, lo:hi], T.lsc[:, lo:hi], T.tq[:, lo:hi], T.tsc[:, lo:hi], sem["arr%d" % k])
 
     sy.wait_ge(sem.add, 4 * (N - 1))
     sy.dma_start(T.y[:], T.yf[:]).then_inc(sem.ydone, 16)
     sy.wait_ge(sem.ydone, 16)
-    g.wait_ge(sem.sent, 2 * n_out * (N - 1))
+    g.wait_ge(sem.sent, 2 * n_out * N)

from concourse.mybir import dt, AluOpType, ActivationFunctionType

N = 6
W = 512
NC = 128
C = 0.031
NS = N - 1

SCRATCH = {
    "abf": ("sbuf", [128, 2 * W], "bfloat16"),
    "bbf": ("sbuf", [128, N * W], "bfloat16"),
    "aq": ("sbuf", [128, 2 * NC], "float8_e4m3fn_x4"),
    "asc": ("sbuf", [128, 2 * NC], "uint8"),
    "bq": ("sbuf", [128, N * NC], "float8_e4m3fn_x4"),
    "bsc": ("sbuf", [128, N * NC], "uint8"),
    "pmj": ("sbuf", [128, NC], "float32"),
    "wbf": ("sbuf", [128, W + 4], "bfloat16"),
    "sq": ("sbuf", [128, 3 * NC], "float8_e4m3fn_x4"),
    "ssc": ("sbuf", [128, 3 * NC], "uint8"),
    "xq": ("sbuf", [128, NC], "float8_e4m3fn_x4"),
    "xsc": ("sbuf", [128, NC], "uint8"),
    "pq": ("sbuf", [128, NC], "float8_e4m3fn_x4"),
    "psc": ("sbuf", [128, NC], "uint8"),
    "rf": ("sbuf", [128, 4 * NS * NC], "float32"),
    "tbf": ("sbuf", [128, NS * W], "bfloat16"),
    "tq": ("sbuf", [128, NS * NC], "float8_e4m3fn_x4"),
    "tsc": ("sbuf", [128, NS * NC], "uint8"),
    "lq": ("sbuf", [128, NS * NC], "float8_e4m3fn_x4"),
    "lsc": ("sbuf", [128, NS * NC], "uint8"),
    "yf": ("sbuf", [128, W], "float32"),
    "pz": ("psum", [128, 4 * 512], "float32"),
    "pd": ("psum", [128, 4 * 512], "float32"),
}

SEMAPHORES = (
    ["la0", "la1", "iot", "zero", "wsel", "qx", "arrs", "qa0", "qa1", "act1", "qs", "add", "qt", "sent", "ydone"]
    + ["lb%d" % i for i in (1, 2, 3, 4)]
    + ["qb%d" % i for i in (1, 2, 3, 4)]
    + ["z%d%d" % (i, j) for i in (1, 2, 3, 4) for j in (0, 1)]
    + ["r%d" % i for i in (2, 3, 4)]
    + ["d%d" % b for b in range(4)]
    + ["arr%d" % k for k in range(1, N)]
)

GROUP = {1: (5, 6), 2: (4, 5), 3: (2, 4), 4: (0, 2)}
BANK = {1: 0, 2: 2, 3: 0, 4: 2}
GROUP_OF_STEP = {1: 1, 2: 2, 3: 3, 4: 3, 5: 4, 6: 4}


def _count(mask):
    return sum((mask >> e) & 1 for e in range(16))


def rank_program(g, core, T, topo):
    r = T.rank_of(core)
    if r is None:
        return
    sem = T.sem
    v, pe, sc, sy = g.vector, g.tensor, g.scalar, g.sync
    nxt, prv = T.cores[(r + 1) % N], T.cores[(r - 1) % N]
    out_mask = topo.mask(core, nxt)
    n_out, n_in = _count(out_mask), _count(topo.mask(prv, core))
    rid, pid = topo.addr(nxt, core)
    relu = ActivationFunctionType.Relu

    def load(queue, gi):
        s0, s1 = GROUP[gi]
        n, s = 0, s0
        while s < s1:
            c, e = (r + s) % N, s + 1
            while e < s1 and (r + e) % N == c + (e - s):
                e += 1
            queue.dma_start(T.bbf[:, W * s:W * e], T.b[:, W * c:W * (c + e - s)]).then_inc(sem["lb%d" % gi], 16)
            n, s = n + 16, e
        return n

    def quant_b(gi):
        s0, s1 = GROUP[gi]
        v.wait_ge(sem["lb%d" % gi], loaded[gi])
        v.quantize_mx(T.bq[:, NC * s0:NC * s1], T.bsc[:, NC * s0:NC * s1],
                      T.bbf[:, W * s0:W * s1]).then_inc(sem["qb%d" % gi], 1)

    def zview(gi, i):
        s0, s1 = GROUP[gi]
        col = 512 * (BANK[gi] + i)
        return T.pz[:, col:col + NC * (s1 - s0)]

    def products(gi):
        s0, s1 = GROUP[gi]
        pe.wait_ge(sem["qb%d" % gi], 1)
        for i in (0, 1):
            if gi == 1:
                pe.wait_ge(sem["qa%d" % i], 1)
            pe.matmul_mx(zview(gi, i), T.aq[:, NC * i:NC * (i + 1)], T.asc[:, NC * i:NC * (i + 1)],
                         T.bq[:, NC * s0:NC * s1], T.bsc[:, NC * s0:NC * s1], True, True).then_inc(sem["z%d%d" % (gi, i)], 1)

    def rview(b, s0, s1):
        return T.rf[:, NS * NC * b + NC * s0:NS * NC * b + NC * s1]

    def parts(gi):
        s0, s1 = GROUP[gi]
        for i in (0, 1):
            sc.wait_ge(sem["z%d%d" % (gi, i)], 1)
            for j, f in ((0, C), (1, -C)):
                sc.activation(rview(2 * i + j, s0, s1), zview(gi, i), relu, scale=f).then_inc(sem["r%d" % gi], 1)

    def send(dq, dsc, q, s_, arrival):
        g.remote_dma(out_ap=dq.bitcast(dt.uint8), in_ap=q.bitcast(dt.uint8),
                     remote_sem=arrival, local_sem=sem.sent, pid=pid, routing_id=rid, dma_engine_mask=out_mask)
        g.remote_dma(out_ap=dsc, in_ap=s_,
                     remote_sem=arrival, local_sem=sem.sent, pid=pid, routing_id=rid, dma_engine_mask=out_mask)

    def pick(b):
        if b < 3:
            return T.sq[:, NC * b:NC * (b + 1)], T.ssc[:, NC * b:NC * (b + 1)]
        return T.pq[:], T.psc[:]

    loaded = {}
    sy.dma_start(T.abf[:, 0:W], T.a[:, 0:W]).then_inc(sem.la0, 16)
    loaded[1] = load(sc, 1)
    sy.dma_start(T.abf[:, W:2 * W], T.a[:, W:2 * W]).then_inc(sem.la1, 16)
    loaded[2] = load(sc, 2)
    loaded[3] = load(sy, 3)
    loaded[4] = load(sc, 4)

    g.iota(T.pmj[:], [[-1, NC]], 0, 1, allow_small_or_imprecise_dtypes=True).then_inc(sem.iot, 1)
    v.memset(T.wbf[:], 0.0).then_inc(sem.zero, 1)
    v.wait_ge(sem.zero, 1)
    v.wait_ge(sem.iot, 1)
    v.tensor_scalar(T.wbf[:, 3:W + 3:4], T.pmj[:], 0.0, None, AluOpType.is_equal).then_inc(sem.wsel, 1)
    v.wait_ge(sem.wsel, 1)
    v.quantize_mx(T.xq[:], T.xsc[:], T.wbf[:, 0:W]).then_inc(sem.qx, 1)
    g.wait_ge(sem.qx, 1)
    send(T.pq[:], T.psc[:], T.xq[:], T.xsc[:], sem.arrs)

    quant_b(1)
    for i in (0, 1):
        v.wait_ge(sem["la%d" % i], 16)
        v.quantize_mx(T.aq[:, NC * i:NC * (i + 1)], T.asc[:, NC * i:NC * (i + 1)],
                      T.abf[:, W * i:W * (i + 1)]).then_inc(sem["qa%d" % i], 1)
    products(1)
    v.wait_ge(sem.z10, 1)
    v.tensor_scalar(T.tbf[:, 0:W:4], zview(1, 0), 0.0, C, AluOpType.max, AluOpType.mult).then_inc(sem.act1, 1)
    v.tensor_scalar(T.tbf[:, 1:W:4], zview(1, 0), -C, 0.0, AluOpType.mult, AluOpType.max).then_inc(sem.act1, 1)
    sc.wait_ge(sem.z11, 1)
    sc.activation(T.tbf[:, 2:W:4], zview(1, 1), relu, scale=C).then_inc(sem.act1, 1)
    sc.activation(T.tbf[:, 3:W:4], zview(1, 1), relu, scale=-C).then_inc(sem.act1, 1)
    v.wait_ge(sem.act1, 4)
    v.quantize_mx(T.tq[:, 0:NC], T.tsc[:, 0:NC], T.tbf[:, 0:W]).then_inc(sem.qt, 1)

    quant_b(2)
    products(2)
    parts(2)
    for b in range(3):
        q, s_ = pick(b)
        v.quantize_mx(q, s_, T.wbf[:, 3 - b:3 - b + W]).then_inc(sem.qs, 1)
    quant_b(3)
    pe.wait_ge(sem.act1, 4)
    products(3)
    parts(3)

    for k in range(2, N + 1):
        s = N - k
        lo, hi = NC * (k - 2), NC * (k - 1)
        pe.wait_ge(sem["arr%d" % (k - 1)], 2 * n_in)
        if k == 2:
            pe.wait_ge(sem.qs, 3)
            pe.wait_ge(sem.arrs, 2 * n_in)
        else:
            pe.wait_ge(sem.add, 4 * (k - 2))
        for b in range(4):
            q, s_ = pick(b)
            pe.matmul_mx(T.pd[:, 512 * b:512 * b + NC], q, s_,
                         T.lq[:, lo:hi], T.lsc[:, lo:hi], True, True).then_inc(sem["d%d" % b], 1)
        v.wait_ge(sem["r%d" % GROUP_OF_STEP[k]], 4)
        for b in range(4):
            out = T.tbf[:, W * (k - 1) + b:W * k:4] if k < N else T.yf[:, b:W:4]
            v.wait_ge(sem["d%d" % b], k - 1)
            v.tensor_tensor(out, T.pd[:, 512 * b:512 * b + NC], rview(b, s, s + 1), AluOpType.add).then_inc(sem.add, 1)
        if k < N:
            v.wait_ge(sem.add, 4 * (k - 1))
            v.quantize_mx(T.tq[:, NC * (k - 1):NC * k], T.tsc[:, NC * (k - 1):NC * k],
                          T.tbf[:, W * (k - 1):W * k]).then_inc(sem.qt, 1)
        if k == 2:
            quant_b(4)
            pe.wait_ge(sem.r2, 4)
            products(4)
            parts(4)

    for k in range(1, N):
        lo, hi = NC * (k - 1), NC * k
        g.wait_ge(sem.qt, k)
        send(T.lq[:, lo:hi], T.lsc[:, lo:hi], T.tq[:, lo:hi], T.tsc[:, lo:hi], sem["arr%d" % k])

    sy.wait_ge(sem.add, 4 * (N - 1))
    sy.dma_start(T.y[:], T.yf[:]).then_inc(sem.ydone, 16)
    sy.wait_ge(sem.ydone, 16)
    g.wait_ge(sem.sent, 2 * n_out * N)
